import numpy as np
import ml_dtypes


def mxq(x, axis, fmt="e4m3"):
    dtype, down = {"e4m3": (ml_dtypes.float8_e4m3fn, 7), "e5m2": (ml_dtypes.float8_e5m2, 14)}[fmt]
    v = np.moveaxis(np.asarray(x, np.float32).astype(ml_dtypes.bfloat16).astype(np.float64), axis, -1)
    blocks = v.reshape(v.shape[:-1] + (-1, 32))
    amax = np.abs(blocks).max(-1, keepdims=True)
    byte = np.maximum(np.where(amax > 0, np.frexp(amax)[1] - 1 + 127, 0) - down, 1)
    scale = np.exp2(byte - 127.0)
    codes = (blocks / scale).astype(np.float32).astype(dtype).astype(np.float64)
    return np.moveaxis((codes * scale).reshape(v.shape), -1, axis)


WIDE = False


def mx_kscale(k):
    if not WIDE:
        return np.ones(k)
    levels = np.array([10, -10, 5, -5, 0])
    if k % 512:
        return np.exp2(np.random.permutation(np.resize(levels, k // 32))).repeat(32)
    a = np.empty((k // 512, 16))
    for p in range(k // 512):
        a[p, :8] = np.random.permutation(np.resize(levels, 8))
        for g in range(8):
            far = levels[np.abs(levels - a[p, g]) >= 10]
            a[p, g + 8] = far[np.random.randint(len(far))]
    return np.exp2(a.ravel()).repeat(32)


def f64(x):
    return np.asarray(x).astype(np.float64)


def striped(idx):
    return np.tile(idx.reshape(-1, 16).T, (8, 1)).astype(np.uint16)


def unstriped(offs):
    return offs[:16].T.reshape(-1).astype(np.int64)


E2M1 = np.array([0.0, 0.5, 1.0, 1.5, 2.0, 3.0, 4.0, 6.0, -0.0, -0.5, -1.0, -1.5, -2.0, -3.0, -4.0, -6.0])


def pack_weight(w, fmt):
    k, n = w.shape
    w = f64(np.asarray(w, np.float32).astype(ml_dtypes.bfloat16)).reshape(k // 32, 32, n)
    amax = np.abs(w).max(1)
    if fmt == "e4m3":
        byte = np.frexp(amax)[1] - 1 + 127 - 7
    else:
        mant, ex = np.frexp(amax / 6.0)
        byte = np.where(mant > 0.5, ex, ex - 1) + 127
    byte = np.clip(np.where(amax > 0, byte, 1), 1, 254)
    scaled = (w * np.exp2(127.0 - byte)[:, None, :]).reshape(k, n).astype(np.float32)
    by_word = np.ascontiguousarray(scaled.reshape(k // 512, 128, 4, n).transpose(0, 1, 3, 2))
    if fmt == "e4m3":
        words = by_word.astype(ml_dtypes.float8_e4m3fn).view(np.uint8)
    else:
        c = by_word.astype(ml_dtypes.float4_e2m1fn).view(np.uint8) & 0xF
        words = (c[..., 0::2] | (c[..., 1::2] << 4)).reshape(k // 512, 128, 2 * n)
    return np.ascontiguousarray(words), np.ascontiguousarray(byte.astype(np.uint8).reshape(k // 512, 16, n))


def unpack_weight(words, scales, fmt):
    g, _, n = scales.shape
    words = np.ascontiguousarray(words).reshape(g, 128, n, -1)
    if fmt == "e4m3":
        vals = words.view(ml_dtypes.float8_e4m3fn).astype(np.float64)
    else:
        nib = np.empty((g, 128, n, 4), np.uint8)
        nib[..., 0::2] = words & 0xF
        nib[..., 1::2] = words >> 4
        vals = E2M1[nib]
    vals = vals * np.repeat(np.exp2(scales.astype(np.float64) - 127.0), 8, axis=1)[..., None]
    return vals.transpose(0, 1, 3, 2).reshape(g * 512, n)


def planes(y):
    n, m = y.shape
    v = y.astype(np.float32).astype(ml_dtypes.bfloat16).astype(np.float64).reshape(n // 32, 32, m)
    top = np.abs(v).max(1)
    byte = np.clip(np.where(top > 0, np.frexp(top)[1] - 1 + 127 - 7, 1), 1, 254)
    codes = (v * np.exp2(127.0 - byte)[:, None, :]).reshape(n, m).astype(np.float32).astype(ml_dtypes.float8_e4m3fn).view(np.uint8)
    words = codes.reshape(n // 512, 128, 4, m).transpose(0, 1, 3, 2)
    return np.ascontiguousarray(words), np.ascontiguousarray(byte.astype(np.uint8).reshape(n // 512, 16, m))


def d_relu2(v):
    return 2.0 * np.maximum(v, 0.0)


K, T, E, C, H, N = 512, 768, 6, 128, 512, 1024


def by_expert(wq, xq):
    return np.concatenate([wq[e].T @ xq[:, e * C:(e + 1) * C] for e in range(E)], axis=1)


def setup_inputs():
    n = np.random.standard_normal
    s = mx_kscale(K)
    v = mx_kscale(N)
    u = mx_kscale(H)
    slot_token = np.random.permutation(T)[:E * C]
    w_slot = np.random.uniform(0.2, 1.0, E * C)
    x = pack_weight(n((K, T)) * s[:, None], "e4m3")
    dy = pack_weight(n((N, T)) * v[:, None], "e4m3")
    m1 = n((E, K, H))
    w1 = [pack_weight(m, "e2m1") for m in m1 / np.sqrt(K) / s[None, :, None]]
    w2t = [pack_weight(m, "e2m1") for m in n((E, N, H)) / np.sqrt(N) / v[None, :, None] * u]
    w1t = [pack_weight(m, "e2m1") for m in m1.transpose(0, 2, 1) / np.sqrt(H) / u[None, :, None]]
    return {
        "x_words": x[0],
        "x_scales": x[1],
        "dy_words": dy[0],
        "dy_scales": dy[1],
        "w1_words": np.stack([m[0] for m in w1]),
        "w1_scales": np.stack([m[1] for m in w1]),
        "w2t_words": np.stack([m[0] for m in w2t]),
        "w2t_scales": np.stack([m[1] for m in w2t]),
        "w1t_words": np.stack([m[0] for m in w1t]),
        "w1t_scales": np.stack([m[1] for m in w1t]),
        "gate": (np.tile(w_slot, (128, 1))).astype(np.float32),
        "offs": striped(slot_token),
    }


def reference(x_words, x_scales, dy_words, dy_scales, w1_words, w1_scales, w2t_words, w2t_scales, w1t_words, w1t_scales, gate, offs):
    w1 = np.stack([unpack_weight(w1_words[e], w1_scales[e], "e2m1") for e in range(E)])
    w2t = np.stack([unpack_weight(w2t_words[e], w2t_scales[e], "e2m1") for e in range(E)])
    w1t = np.stack([unpack_weight(w1t_words[e], w1t_scales[e], "e2m1") for e in range(E)])
    idx = unstriped(offs)
    xq = unpack_weight(x_words, x_scales, "e4m3")[:, idx]
    gq = unpack_weight(dy_words, dy_scales, "e4m3")[:, idx]
    dh = f64(gate[:1]) * by_expert(w2t, gq)
    a = by_expert(w1, xq)
    dx = by_expert(w1t, mxq(dh * d_relu2(a), 0, "e4m3"))
    out = np.zeros((K, T))
    out[:, idx] = dx
    out_0 = out
    return (out_0,) + planes(out_0)

@@ -1,0 +1,195 @@
+from contextlib import ExitStack
+
+import concourse.mybir as mybir
+from concourse.masks import make_identity
+
+K, T, E, C, H, N = 512, 768, 6, 128, 512, 1024
+FLOPS = 2 * E * C * (K * H + N * H + H * K)
+
+F32 = mybir.dt.float32
+BF16 = mybir.dt.bfloat16
+I32 = mybir.dt.int32
+U32 = mybir.dt.uint32
+U16 = mybir.dt.uint16
+U8 = mybir.dt.uint8
+FP8X4 = mybir.dt.float8_e4m3fn_x4
+FP4X4 = mybir.dt.float4_e2m1fn_x4
+ACT = mybir.ActivationFunctionType
+ALU = mybir.AluOpType
+
+P = 128
+PACK = 4
+QUADS = 4
+GROUP = 2
+GROUPS = E // GROUP
+LIST_ROWS = 16
+VECTOR_COLS = 512
+
+
+def tile_moe_rec_mlp_relu2_kernel(
+    tc, x_words, x_scales, dy_words, dy_scales, w1_words, w1_scales, w2t_words, w2t_scales,
+    w1t_words, w1t_scales, gate, offs, out_0, out_1, out_2,
+):
+    nc = tc.nc
+    with ExitStack() as ctx:
+        keep = ctx.enter_context(tc.tile_pool(name="keep", bufs=1))
+        picked = ctx.enter_context(tc.tile_pool(name="picked", bufs=2))
+        work = ctx.enter_context(tc.tile_pool(name="work", bufs=2))
+        psum2 = ctx.enter_context(tc.psum_pool(name="psum2", bufs=2))
+        psum1 = ctx.enter_context(tc.psum_pool(name="psum1", bufs=1))
+
+        offsets = keep.tile([P, E * C // LIST_ROWS], U16, name="offsets")
+        x_tab = keep.tile([P, T], I32, name="x_tab", align_bytes=64)
+        dy_tab = keep.tile([P, 2, T], I32, name="dy_tab", align_bytes=64)
+        xs_tab = keep.tile([P, 1, T], U8, name="xs_tab", align_bytes=64)
+        dys_tab = keep.tile([P, 2, T], U8, name="dys_tab", align_bytes=64)
+        w1_s = keep.tile([P, E, H], U8, name="w1_s", align_bytes=64)
+        w2_s = keep.tile([P, 2 * E, H], U8, name="w2_s", align_bytes=64)
+        w1t_s = keep.tile([P, E, K], U8, name="w1t_s", align_bytes=64)
+
+        for plane in (xs_tab, dys_tab, w1_s, w2_s, w1t_s):
+            nc.vector.memset(plane[:].bitcast(I32), 0)
+
+        def load_scales(plane, rows):
+            for q in range(QUADS):
+                nc.sync.dma_start(out=plane[32 * q : 32 * q + 4].bitcast(I32), in_=rows[4 * q : 4 * q + 4].bitcast(I32))
+
+        def load_weights(words, g, label):
+            passes = words.shape[1]
+            tile = keep.tile([P, GROUP * passes, 2 * H], U8, name="%s_%d" % (label, g), align_bytes=64)
+            src = words[g * GROUP : (g + 1) * GROUP].rearrange("e s p b -> p (e s) b")
+            nc.sync.dma_start(out=tile[:].bitcast(I32), in_=src.bitcast(I32))
+            return tile
+
+        nc.sync.dma_start(offsets[:], offs)
+        nc.sync.dma_start(out=x_tab[:], in_=x_words[0].rearrange("p t d -> p (t d)").bitcast(I32))
+        nc.sync.dma_start(out=dy_tab[:], in_=dy_words.rearrange("s p t d -> p s (t d)").bitcast(I32))
+        load_scales(xs_tab, x_scales.rearrange("s b t -> b s t"))
+        load_scales(dys_tab, dy_scales.rearrange("s b t -> b s t"))
+        load_scales(w1_s, w1_scales.rearrange("e s b i -> b (e s) i"))
+        load_scales(w2_s, w2t_scales.rearrange("e s b i -> b (e s) i"))
+        w1_w, w2_w, w1t_w = {}, {}, {}
+        for g in range(2):
+            w1_w[g] = load_weights(w1_words, g, "w1")
+            w2_w[g] = load_weights(w2t_words, g, "w2")
+        load_scales(w1t_s, w1t_scales.rearrange("e s b i -> b (e s) i"))
+        w1t_w[0] = load_weights(w1t_words, 0, "w1t")
+        w1_w[2] = load_weights(w1_words, 2, "w1")
+        w2_w[2] = load_weights(w2t_words, 2, "w2")
+        w1t_w[1] = load_weights(w1t_words, 1, "w1t")
+        w1t_w[2] = load_weights(w1t_words, 2, "w1t")
+
+        gate_rows = keep.tile([P, C], F32, name="gate_rows")
+        nc.gpsimd.memset(gate_rows[:], 0.0)
+        nc.gpsimd.dma_start(out=gate_rows[0:E, :], in_=gate[0:1, :].rearrange("o (e c) -> (o e) c", c=C))
+        ident = keep.tile([P, P], F32, name="ident")
+        make_identity(nc, ident[:])
+        gate_ps = psum1.tile([P, 2, P], F32, name="gate_ps", tag="da_t")
+        nc.tensor.transpose(gate_ps[:, 0, :], gate_rows[:], ident[:])
+        gate2 = keep.tile([P, 8], F32, name="gate2")
+        nc.scalar.activation(gate2[:], gate_ps[:, 0, 0:8], ACT.Copy, scale=2.0)
+
+        dx = keep.tile([P, PACK, E * C], F32, name="dx")
+        windows = [keep.tile([P, T], F32, name="window_%d" % t) for t in range(PACK)]
+
+        def gather(g):
+            cols = GROUP * C
+            piece = offsets[:, g * cols // LIST_ROWS : (g + 1) * cols // LIST_ROWS]
+            got = []
+            tables = [(x_tab[:], xs_tab[:, 0, :]), (dy_tab[:, 0, :], dys_tab[:, 0, :]), (dy_tab[:, 1, :], dys_tab[:, 1, :])]
+            for n, (words, scales) in enumerate(tables):
+                w = picked.tile([P, cols], U32, name="words_%d" % n, align_bytes=64)
+                nc.vector.tensor_copy(w[:], words.bitcast(U32).indirect(piece))
+                s = picked.tile([P, cols], U8, name="scales_%d" % n, align_bytes=64)
+                nc.vector.tensor_copy(s[:], scales.indirect(piece))
+                got.append((w, s))
+            return got
+
+        def product(out, lhs, slots, w_tile, w_row, s_tile, s_row, start, stop):
+            nc.tensor.matmul_mx(
+                out=out, lhsT=lhs[0][:, slots].bitcast(FP8X4), lhsT_scale=lhs[1][:, slots],
+                rhs=w_tile[:, w_row, :].bitcast(FP4X4), rhs_scale=s_tile[:, s_row, :], start=start, stop=stop,
+            )
+
+        def hidden(e, got):
+            g, u = divmod(e, GROUP)
+            slots = slice(u * C, (u + 1) * C)
+            a_ps = psum2.tile([P, H], F32, name="a_ps")
+            product(a_ps[:], got[0], slots, w1_w[g], u, w1_s, e, True, True)
+            dh_ps = psum2.tile([P, H], F32, name="dh_ps")
+            for s in range(2):
+                product(dh_ps[:], got[1 + s], slots, w2_w[g], 2 * u + s, w2_s, 2 * e + s, s == 0, s == 1)
+            relu = work.tile([P, H], F32, name="relu")
+            nc.scalar.activation(relu[:], a_ps[:], ACT.Relu)
+            da = work.tile([P, H], BF16, name="da", align_bytes=64)
+            nc.vector.scalar_tensor_tensor(da[:], dh_ps[:], gate2[:, e : e + 1], relu[:], ALU.mult, ALU.mult)
+            return da
+
+        def quantise(da):
+            words = da[:].bitcast(F32)
+            da_ps = psum1.tile([P, 2, C], F32, name="da_ps", tag="da_t")
+            for u in range(2):
+                nc.tensor.transpose(da_ps[:, u, :], words[:, u : H // 2 : 2], ident[:])
+            grouped = work.tile([P, C * PACK], BF16, name="grouped", align_bytes=64)
+            nc.scalar.copy(grouped[:].bitcast(F32).rearrange("p (c u) -> p c u", u=2), da_ps[:].rearrange("p u c -> p c u"))
+            codes = work.tile([P, C], U32, name="codes", align_bytes=64)
+            scales = work.tile([P, C], U8, name="code_scales", align_bytes=64)
+            nc.vector.quantize_mx(out=codes[:].bitcast(FP8X4), scales=scales[:], in_=grouped[:])
+            return codes, scales
+
+        def back(e, da_q):
+            g, u = divmod(e, GROUP)
+            dxt_ps = psum1.tile([P, K], F32, name="dxt_ps")
+            product(dxt_ps[:], da_q, slice(0, C), w1t_w[g], u, w1t_s, e, True, True)
+            dxt = work.tile([P, PACK, P], F32, name="dxt")
+            nc.scalar.copy(dxt[:], dxt_ps[:].rearrange("c (m t) -> c t m", t=PACK))
+            dx_ps = psum2.tile([P, PACK, C], F32, name="dx_ps")
+            for t in range(PACK):
+                nc.tensor.transpose(dx_ps[:, t, :], dxt[:, t, :], ident[:])
+            nc.scalar.copy(dx[:, :, e * C : (e + 1) * C], dx_ps[:])
+
+        def scatter(t, first, last):
+            piece = offsets[:, first * C // LIST_ROWS : (last + 1) * C // LIST_ROWS]
+            nc.vector.tensor_copy(windows[t][:].indirect(piece), dx[:, t, first * C : (last + 1) * C])
+
+        tail_from = [5, 4, 2, 2]
+        got, da, da_q = {}, {}, {}
+        got[0] = gather(0)
+        got[1] = gather(1)
+        for step in range(E + 3):
+            if step < E:
+                da[step] = hidden(step, got[step // GROUP])
+            if step == GROUP - 1:
+                got[2] = gather(2)
+            if 0 <= step - 1 < E:
+                da_q[step - 1] = quantise(da[step - 1])
+            if 0 <= step - 2 < E:
+                back(step - 2, da_q[step - 2])
+            e = step - 3
+            if 0 <= e < E - 1:
+                for t in range(PACK):
+                    if e < tail_from[t]:
+                        scatter(t, e, e)
+
+        rounded = keep.tile([P, T, PACK], BF16, name="rounded", align_bytes=64)
+        y_codes = keep.tile([P, T * PACK], U8, name="y_codes", align_bytes=64)
+        y_scales = keep.tile([P, T], U8, name="y_scales", align_bytes=64)
+        out_rows = out_0.rearrange("(p t) c -> p t c", t=PACK)
+        for t in range(PACK):
+            scatter(t, tail_from[t], E - 1)
+            nc.sync.dma_start(out=out_rows[:, t, :], in_=windows[t][:])
+            if t < 2:
+                nc.scalar.copy(rounded[:, :, t], windows[t][:])
+            elif t == 2:
+                nc.scalar.copy(rounded[:, :, 2:4], windows[t][:].unsqueeze(2).to_broadcast([P, T, 2]))
+            else:
+                nc.scalar.copy(rounded[:, VECTOR_COLS:, t], windows[t][:, VECTOR_COLS:])
+                nc.vector.tensor_copy(rounded[:, :VECTOR_COLS, t], windows[t][:, :VECTOR_COLS])
+        flat = rounded[:].rearrange("p c t -> p (c t)")
+        words_out = out_1[0].rearrange("p c d -> p (c d)")
+        for a, b in ((VECTOR_COLS, T), (0, VECTOR_COLS)):
+            nc.vector.quantize_mx(out=y_codes[:, PACK * a : PACK * b].bitcast(FP8X4), scales=y_scales[:, a:b], in_=flat[:, PACK * a : PACK * b])
+            nc.sync.dma_start(out=words_out[:, PACK * a : PACK * b].bitcast(I32), in_=y_codes[:, PACK * a : PACK * b].bitcast(I32))
+        for q in range(QUADS):
+            queue = nc.sync if q % 2 == 0 else nc.scalar
+            queue.dma_start(out=out_2[0, 4 * q : 4 * q + 4, :].bitcast(I32), in_=y_scales[32 * q : 32 * q + 4, :].bitcast(I32))

@@ -24,6 +24,7 @@ GROUP = 2
 GROUPS = E // GROUP
 LIST_ROWS = 16
 VECTOR_COLS = 512
+AHEAD = 3
 
 
 def tile_moe_rec_mlp_relu2_kernel(
@@ -33,10 +34,9 @@ def tile_moe_rec_mlp_relu2_kernel(
     nc = tc.nc
     with ExitStack() as ctx:
         keep = ctx.enter_context(tc.tile_pool(name="keep", bufs=1))
-        picked = ctx.enter_context(tc.tile_pool(name="picked", bufs=2))
+        picked = ctx.enter_context(tc.tile_pool(name="picked", bufs=AHEAD))
         work = ctx.enter_context(tc.tile_pool(name="work", bufs=2))
-        psum2 = ctx.enter_context(tc.psum_pool(name="psum2", bufs=2))
-        psum1 = ctx.enter_context(tc.psum_pool(name="psum1", bufs=1))
+        psum = ctx.enter_context(tc.psum_pool(name="psum", bufs=1))
 
         offsets = keep.tile([P, E * C // LIST_ROWS], U16, name="offsets")
         x_tab = keep.tile([P, T], I32, name="x_tab", align_bytes=64)
@@ -47,44 +47,53 @@ def tile_moe_rec_mlp_relu2_kernel(
         w2_s = keep.tile([P, 2 * E, H], U8, name="w2_s", align_bytes=64)
         w1t_s = keep.tile([P, E, K], U8, name="w1t_s", align_bytes=64)
 
-        for plane in (xs_tab, dys_tab, w1_s, w2_s, w1t_s):
+        for plane in (xs_tab, dys_tab):
+            nc.gpsimd.memset(plane[:].bitcast(I32), 0)
+        for plane in (w2_s, w1_s, w1t_s):
             nc.vector.memset(plane[:].bitcast(I32), 0)
 
-        def load_scales(plane, rows):
-            for q in range(QUADS):
-                nc.sync.dma_start(out=plane[32 * q : 32 * q + 4].bitcast(I32), in_=rows[4 * q : 4 * q + 4].bitcast(I32))
+        def load_scales(plane, rows, first, count):
+            for r in range(PACK):
+                nc.sync.dma_start(
+                    out=plane[r:P:32, first : first + count, :].bitcast(I32),
+                    in_=rows[r:16:4, first : first + count, :].bitcast(I32),
+                )
 
-        def load_weights(words, g, label):
+        def load_weights(held, words, first, count, label):
             passes = words.shape[1]
-            tile = keep.tile([P, GROUP * passes, 2 * H], U8, name="%s_%d" % (label, g), align_bytes=64)
-            src = words[g * GROUP : (g + 1) * GROUP].rearrange("e s p b -> p (e s) b")
+            tile = keep.tile([P, count * passes, 2 * H], U8, name="%s_%d" % (label, first), align_bytes=64)
+            src = words[first : first + count].rearrange("e s p b -> p (e s) b")
             nc.sync.dma_start(out=tile[:].bitcast(I32), in_=src.bitcast(I32))
-            return tile
+            for u in range(count):
+                held[first + u] = [tile[:, u * passes + s, :] for s in range(passes)]
 
         nc.sync.dma_start(offsets[:], offs)
+        w1_w, w2_w, w1t_w = {}, {}, {}
+        w1_rows = w1_scales.rearrange("e s b i -> b (e s) i")
+        w2_rows = w2t_scales.rearrange("e s b i -> b (e s) i")
+        w1t_rows = w1t_scales.rearrange("e s b i -> b (e s) i")
+        load_scales(xs_tab, x_scales.rearrange("s b t -> b s t"), 0, 1)
         nc.sync.dma_start(out=x_tab[:], in_=x_words[0].rearrange("p t d -> p (t d)").bitcast(I32))
         nc.sync.dma_start(out=dy_tab[:], in_=dy_words.rearrange("s p t d -> p s (t d)").bitcast(I32))
-        load_scales(xs_tab, x_scales.rearrange("s b t -> b s t"))
-        load_scales(dys_tab, dy_scales.rearrange("s b t -> b s t"))
-        load_scales(w1_s, w1_scales.rearrange("e s b i -> b (e s) i"))
-        load_scales(w2_s, w2t_scales.rearrange("e s b i -> b (e s) i"))
-        w1_w, w2_w, w1t_w = {}, {}, {}
-        for g in range(2):
-            w1_w[g] = load_weights(w1_words, g, "w1")
-            w2_w[g] = load_weights(w2t_words, g, "w2")
-        load_scales(w1t_s, w1t_scales.rearrange("e s b i -> b (e s) i"))
-        w1t_w[0] = load_weights(w1t_words, 0, "w1t")
-        w1_w[2] = load_weights(w1_words, 2, "w1")
-        w2_w[2] = load_weights(w2t_words, 2, "w2")
-        w1t_w[1] = load_weights(w1t_words, 1, "w1t")
-        w1t_w[2] = load_weights(w1t_words, 2, "w1t")
+        load_scales(dys_tab, dy_scales.rearrange("s b t -> b s t"), 0, 2)
+        load_weights(w2_w, w2t_words, 0, 2, "w2")
+        load_scales(w2_s, w2_rows, 0, 4)
+        load_weights(w1_w, w1_words, 0, 2, "w1")
+        load_scales(w1_s, w1_rows, 0, 6)
+        load_weights(w2_w, w2t_words, 2, 2, "w2")
+        load_scales(w2_s, w2_rows, 4, 8)
+        load_weights(w1t_w, w1t_words, 0, 2, "w1t")
+        load_scales(w1t_s, w1t_rows, 0, 6)
+        load_weights(w1_w, w1_words, 2, 4, "w1")
+        load_weights(w2_w, w2t_words, 4, 2, "w2")
+        load_weights(w1t_w, w1t_words, 2, 4, "w1t")
 
         gate_rows = keep.tile([P, C], F32, name="gate_rows")
         nc.gpsimd.memset(gate_rows[:], 0.0)
         nc.gpsimd.dma_start(out=gate_rows[0:E, :], in_=gate[0:1, :].rearrange("o (e c) -> (o e) c", c=C))
         ident = keep.tile([P, P], F32, name="ident")
         make_identity(nc, ident[:])
-        gate_ps = psum1.tile([P, 2, P], F32, name="gate_ps", tag="da_t")
+        gate_ps = psum.tile([P, 2, P], F32, name="gate_ps", tag="da_t")
         nc.tensor.transpose(gate_ps[:, 0, :], gate_rows[:], ident[:])
         gate2 = keep.tile([P, 8], F32, name="gate2")
         nc.scalar.activation(gate2[:], gate_ps[:, 0, 0:8], ACT.Copy, scale=2.0)
@@ -92,42 +101,39 @@ def tile_moe_rec_mlp_relu2_kernel(
         dx = keep.tile([P, PACK, E * C], F32, name="dx")
         windows = [keep.tile([P, T], F32, name="window_%d" % t) for t in range(PACK)]
 
-        def gather(g):
-            cols = GROUP * C
-            piece = offsets[:, g * cols // LIST_ROWS : (g + 1) * cols // LIST_ROWS]
+        def gather(e):
+            piece = offsets[:, e * C // LIST_ROWS : (e + 1) * C // LIST_ROWS]
+            tables = [(dy_tab[:, 0, :], dys_tab[:, 0, :]), (dy_tab[:, 1, :], dys_tab[:, 1, :]), (x_tab[:], xs_tab[:, 0, :])]
             got = []
-            tables = [(x_tab[:], xs_tab[:, 0, :]), (dy_tab[:, 0, :], dys_tab[:, 0, :]), (dy_tab[:, 1, :], dys_tab[:, 1, :])]
             for n, (words, scales) in enumerate(tables):
-                w = picked.tile([P, cols], U32, name="words_%d" % n, align_bytes=64)
+                w = picked.tile([P, C], U32, name="words_%d" % n, align_bytes=64)
                 nc.vector.tensor_copy(w[:], words.bitcast(U32).indirect(piece))
-                s = picked.tile([P, cols], U8, name="scales_%d" % n, align_bytes=64)
+                s = picked.tile([P, C], U8, name="scales_%d" % n, align_bytes=64)
                 nc.vector.tensor_copy(s[:], scales.indirect(piece))
                 got.append((w, s))
             return got
 
-        def product(out, lhs, slots, w_tile, w_row, s_tile, s_row, start, stop):
+        def product(out, lhs, weight, weight_scales, start, stop):
             nc.tensor.matmul_mx(
-                out=out, lhsT=lhs[0][:, slots].bitcast(FP8X4), lhsT_scale=lhs[1][:, slots],
-                rhs=w_tile[:, w_row, :].bitcast(FP4X4), rhs_scale=s_tile[:, s_row, :], start=start, stop=stop,
+                out=out, lhsT=lhs[0][:].bitcast(FP8X4), lhsT_scale=lhs[1][:],
+                rhs=weight.bitcast(FP4X4), rhs_scale=weight_scales, start=start, stop=stop,
             )
 
-        def hidden(e, got):
-            g, u = divmod(e, GROUP)
-            slots = slice(u * C, (u + 1) * C)
-            a_ps = psum2.tile([P, H], F32, name="a_ps")
-            product(a_ps[:], got[0], slots, w1_w[g], u, w1_s, e, True, True)
-            dh_ps = psum2.tile([P, H], F32, name="dh_ps")
+        def hidden(e):
+            dh_ps = psum.tile([P, H], F32, name="dh_ps", bufs=2)
             for s in range(2):
-                product(dh_ps[:], got[1 + s], slots, w2_w[g], 2 * u + s, w2_s, 2 * e + s, s == 0, s == 1)
-            relu = work.tile([P, H], F32, name="relu")
-            nc.scalar.activation(relu[:], a_ps[:], ACT.Relu)
+                product(dh_ps[:], got[e][s], w2_w[e][s], w2_s[:, 2 * e + s, :], s == 0, s == 1)
+            dh2 = work.tile([P, H], F32, name="dh2", bufs=2)
+            nc.scalar.activation(dh2[:], dh_ps[:], ACT.Copy, scale=gate2[:, e : e + 1])
+            a_ps = psum.tile([P, H], F32, name="a_ps", bufs=2)
+            product(a_ps[:], got[e][2], w1_w[e][0], w1_s[:, e, :], True, True)
             da = work.tile([P, H], BF16, name="da", align_bytes=64)
-            nc.vector.scalar_tensor_tensor(da[:], dh_ps[:], gate2[:, e : e + 1], relu[:], ALU.mult, ALU.mult)
+            nc.vector.scalar_tensor_tensor(da[:], a_ps[:], 0.0, dh2[:], ALU.max, ALU.mult)
             return da
 
         def quantise(da):
             words = da[:].bitcast(F32)
-            da_ps = psum1.tile([P, 2, C], F32, name="da_ps", tag="da_t")
+            da_ps = psum.tile([P, 2, C], F32, name="da_ps", tag="da_t")
             for u in range(2):
                 nc.tensor.transpose(da_ps[:, u, :], words[:, u : H // 2 : 2], ident[:])
             grouped = work.tile([P, C * PACK], BF16, name="grouped", align_bytes=64)
@@ -138,12 +144,11 @@ def tile_moe_rec_mlp_relu2_kernel(
             return codes, scales
 
         def back(e, da_q):
-            g, u = divmod(e, GROUP)
-            dxt_ps = psum1.tile([P, K], F32, name="dxt_ps")
-            product(dxt_ps[:], da_q, slice(0, C), w1t_w[g], u, w1t_s, e, True, True)
+            dxt_ps = psum.tile([P, K], F32, name="dxt_ps", bufs=1)
+            product(dxt_ps[:], da_q, w1t_w[e][0], w1t_s[:, e, :], True, True)
             dxt = work.tile([P, PACK, P], F32, name="dxt")
             nc.scalar.copy(dxt[:], dxt_ps[:].rearrange("c (m t) -> c t m", t=PACK))
-            dx_ps = psum2.tile([P, PACK, C], F32, name="dx_ps")
+            dx_ps = psum.tile([P, PACK, C], F32, name="dx_ps", bufs=2)
             for t in range(PACK):
                 nc.tensor.transpose(dx_ps[:, t, :], dxt[:, t, :], ident[:])
             nc.scalar.copy(dx[:, :, e * C : (e + 1) * C], dx_ps[:])
@@ -152,24 +157,22 @@ def tile_moe_rec_mlp_relu2_kernel(
             piece = offsets[:, first * C // LIST_ROWS : (last + 1) * C // LIST_ROWS]
             nc.vector.tensor_copy(windows[t][:].indirect(piece), dx[:, t, first * C : (last + 1) * C])
 
-        tail_from = [5, 4, 2, 2]
+        tail_from = [5, 4, 3, 2]
+        early = {0: [(0, 0), (1, 0)], 1: [(3, 0)], 2: [(2, 0)], 3: [(1, 1)], 4: [(0, 1)]}
         got, da, da_q = {}, {}, {}
-        got[0] = gather(0)
-        got[1] = gather(1)
-        for step in range(E + 3):
+        for e in range(AHEAD):
+            got[e] = gather(e)
+        for step in range(E + 2):
             if step < E:
-                da[step] = hidden(step, got[step // GROUP])
-            if step == GROUP - 1:
-                got[2] = gather(2)
+                da[step] = hidden(step)
+            if step + AHEAD < E:
+                got[step + AHEAD] = gather(step + AHEAD)
             if 0 <= step - 1 < E:
                 da_q[step - 1] = quantise(da[step - 1])
             if 0 <= step - 2 < E:
                 back(step - 2, da_q[step - 2])
-            e = step - 3
-            if 0 <= e < E - 1:
-                for t in range(PACK):
-                    if e < tail_from[t]:
-                        scatter(t, e, e)
+            for t, first in early.get(step - 3, []):
+                scatter(t, first, step - 3)
 
         rounded = keep.tile([P, T, PACK], BF16, name="rounded", align_bytes=64)
         y_codes = keep.tile([P, T * PACK], U8, name="y_codes", align_bytes=64)
@@ -181,7 +184,8 @@ def tile_moe_rec_mlp_relu2_kernel(
             if t < 2:
                 nc.scalar.copy(rounded[:, :, t], windows[t][:])
             elif t == 2:
-                nc.scalar.copy(rounded[:, :, 2:4], windows[t][:].unsqueeze(2).to_broadcast([P, T, 2]))
+                nc.scalar.copy(rounded[:, :VECTOR_COLS, 2:4], windows[t][:, :VECTOR_COLS].unsqueeze(2).to_broadcast([P, VECTOR_COLS, 2]))
+                nc.scalar.copy(rounded[:, VECTOR_COLS:, t], windows[t][:, VECTOR_COLS:])
             else:
                 nc.scalar.copy(rounded[:, VECTOR_COLS:, t], windows[t][:, VECTOR_COLS:])
                 nc.vector.tensor_copy(rounded[:, :VECTOR_COLS, t], windows[t][:, :VECTOR_COLS])
@@ -192,4 +196,4 @@ def tile_moe_rec_mlp_relu2_kernel(
             nc.sync.dma_start(out=words_out[:, PACK * a : PACK * b].bitcast(I32), in_=y_codes[:, PACK * a : PACK * b].bitcast(I32))
         for q in range(QUADS):
             queue = nc.sync if q % 2 == 0 else nc.scalar
-            queue.dma_start(out=out_2[0, 4 * q : 4 * q + 4, :].bitcast(I32), in_=y_scales[32 * q : 32 * q + 4, :].bitcast(I32))
+            queue.dma_start(out=out_2[0, q:16:4, :].bitcast(I32), in_=y_scales[q:P:32, :].bitcast(I32))

@@ -24,7 +24,9 @@ GROUP = 2
 GROUPS = E // GROUP
 LIST_ROWS = 16
 VECTOR_COLS = 512
-AHEAD = 3
+PIECE = 256
+ALONE = 3
+AHEAD = 2
 
 
 def tile_moe_rec_mlp_relu2_kernel(
@@ -49,6 +51,10 @@ def tile_moe_rec_mlp_relu2_kernel(
 
         for plane in (xs_tab, dys_tab):
             nc.gpsimd.memset(plane[:].bitcast(I32), 0)
+        ident = keep.tile([P, P], F32, name="ident")
+        make_identity(nc, ident[:])
+        gate_rows = keep.tile([P, C], F32, name="gate_rows")
+        nc.vector.memset(gate_rows[:], 0.0)
         for plane in (w2_s, w1_s, w1t_s):
             nc.vector.memset(plane[:].bitcast(I32), 0)
 
@@ -82,17 +88,14 @@ def tile_moe_rec_mlp_relu2_kernel(
         load_scales(w1_s, w1_rows, 0, 6)
         load_weights(w2_w, w2t_words, 2, 2, "w2")
         load_scales(w2_s, w2_rows, 4, 8)
+        load_weights(w1_w, w1_words, 2, 2, "w1")
         load_weights(w1t_w, w1t_words, 0, 2, "w1t")
         load_scales(w1t_s, w1t_rows, 0, 6)
-        load_weights(w1_w, w1_words, 2, 4, "w1")
         load_weights(w2_w, w2t_words, 4, 2, "w2")
+        load_weights(w1_w, w1_words, 4, 2, "w1")
         load_weights(w1t_w, w1t_words, 2, 4, "w1t")
 
-        gate_rows = keep.tile([P, C], F32, name="gate_rows")
-        nc.gpsimd.memset(gate_rows[:], 0.0)
-        nc.gpsimd.dma_start(out=gate_rows[0:E, :], in_=gate[0:1, :].rearrange("o (e c) -> (o e) c", c=C))
-        ident = keep.tile([P, P], F32, name="ident")
-        make_identity(nc, ident[:])
+        nc.scalar.dma_start(out=gate_rows[0:E, :], in_=gate[0:1, :].rearrange("o (e c) -> (o e) c", c=C))
         gate_ps = psum.tile([P, 2, P], F32, name="gate_ps", tag="da_t")
         nc.tensor.transpose(gate_ps[:, 0, :], gate_rows[:], ident[:])
         gate2 = keep.tile([P, 8], F32, name="gate2")
@@ -157,8 +160,7 @@ def tile_moe_rec_mlp_relu2_kernel(
             piece = offsets[:, first * C // LIST_ROWS : (last + 1) * C // LIST_ROWS]
             nc.vector.tensor_copy(windows[t][:].indirect(piece), dx[:, t, first * C : (last + 1) * C])
 
-        tail_from = [5, 4, 3, 2]
-        early = {0: [(0, 0), (1, 0)], 1: [(3, 0)], 2: [(2, 0)], 3: [(1, 1)], 4: [(0, 1)]}
+        tail_from = [E - 1 - t for t in range(PACK)]
         got, da, da_q = {}, {}, {}
         for e in range(AHEAD):
             got[e] = gather(e)
@@ -171,8 +173,13 @@ def tile_moe_rec_mlp_relu2_kernel(
                 da_q[step - 1] = quantise(da[step - 1])
             if 0 <= step - 2 < E:
                 back(step - 2, da_q[step - 2])
-            for t, first in early.get(step - 3, []):
-                scatter(t, first, step - 3)
+            e = step - 3
+            for t in range(PACK):
+                alone = t < ALONE
+                if e == 0 and alone:
+                    scatter(t, 0, 0)
+                elif e == tail_from[t] - 1:
+                    scatter(t, 1 if alone else 0, e)
 
         rounded = keep.tile([P, T, PACK], BF16, name="rounded", align_bytes=64)
         y_codes = keep.tile([P, T * PACK], U8, name="y_codes", align_bytes=64)
@@ -188,10 +195,12 @@ def tile_moe_rec_mlp_relu2_kernel(
                 nc.scalar.copy(rounded[:, VECTOR_COLS:, t], windows[t][:, VECTOR_COLS:])
             else:
                 nc.scalar.copy(rounded[:, VECTOR_COLS:, t], windows[t][:, VECTOR_COLS:])
-                nc.vector.tensor_copy(rounded[:, :VECTOR_COLS, t], windows[t][:, :VECTOR_COLS])
+                for a in range(0, VECTOR_COLS, PIECE):
+                    nc.vector.tensor_copy(rounded[:, a : a + PIECE, t], windows[t][:, a : a + PIECE])
         flat = rounded[:].rearrange("p c t -> p (c t)")
         words_out = out_1[0].rearrange("p c d -> p (c d)")
-        for a, b in ((VECTOR_COLS, T), (0, VECTOR_COLS)):
+        for a in (0, VECTOR_COLS, PIECE):
+            b = a + PIECE
             nc.vector.quantize_mx(out=y_codes[:, PACK * a : PACK * b].bitcast(FP8X4), scales=y_scales[:, a:b], in_=flat[:, PACK * a : PACK * b])
             nc.sync.dma_start(out=words_out[:, PACK * a : PACK * b].bitcast(I32), in_=y_codes[:, PACK * a : PACK * b].bitcast(I32))
         for q in range(QUADS):

@@ -20,12 +20,12 @@ ALU = mybir.AluOpType
 P = 128
 PACK = 4
 QUADS = 4
-GROUP = 2
+GROUP = 3
 GROUPS = E // GROUP
 LIST_ROWS = 16
 VECTOR_COLS = 512
 PIECE = 256
-ALONE = 3
+ALONE = 2
 AHEAD = 2
 
 
@@ -49,18 +49,14 @@ def tile_moe_rec_mlp_relu2_kernel(
         w2_s = keep.tile([P, 2 * E, H], U8, name="w2_s", align_bytes=64)
         w1t_s = keep.tile([P, E, K], U8, name="w1t_s", align_bytes=64)
 
-        for plane in (xs_tab, dys_tab):
+        for plane in (xs_tab, dys_tab,):
             nc.gpsimd.memset(plane[:].bitcast(I32), 0)
-        ident = keep.tile([P, P], F32, name="ident")
-        make_identity(nc, ident[:])
-        gate_rows = keep.tile([P, C], F32, name="gate_rows")
-        nc.vector.memset(gate_rows[:], 0.0)
-        for plane in (w2_s, w1_s, w1t_s):
+        for plane in (w1_s, w2_s, w1t_s,):
             nc.vector.memset(plane[:].bitcast(I32), 0)
 
-        def load_scales(plane, rows, first, count):
+        def load_scales(plane, rows, first, count, queue=nc.sync):
             for r in range(PACK):
-                nc.sync.dma_start(
+                queue.dma_start(
                     out=plane[r:P:32, first : first + count, :].bitcast(I32),
                     in_=rows[r:16:4, first : first + count, :].bitcast(I32),
                 )
@@ -82,20 +78,22 @@ def tile_moe_rec_mlp_relu2_kernel(
         nc.sync.dma_start(out=x_tab[:], in_=x_words[0].rearrange("p t d -> p (t d)").bitcast(I32))
         nc.sync.dma_start(out=dy_tab[:], in_=dy_words.rearrange("s p t d -> p s (t d)").bitcast(I32))
         load_scales(dys_tab, dy_scales.rearrange("s b t -> b s t"), 0, 2)
-        load_weights(w2_w, w2t_words, 0, 2, "w2")
-        load_scales(w2_s, w2_rows, 0, 4)
         load_weights(w1_w, w1_words, 0, 2, "w1")
         load_scales(w1_s, w1_rows, 0, 6)
+        load_weights(w2_w, w2t_words, 0, 2, "w2")
+        load_scales(w2_s, w2_rows, 0, 12)
+        gate_rows = keep.tile([P, C], F32, name="gate_rows")
+        nc.gpsimd.memset(gate_rows[:], 0.0)
+        nc.gpsimd.dma_start(out=gate_rows[0:E, :], in_=gate[0:1, :].rearrange("o (e c) -> (o e) c", c=C))
+        ident = keep.tile([P, P], F32, name="ident")
+        make_identity(nc, ident[:])
         load_weights(w2_w, w2t_words, 2, 2, "w2")
-        load_scales(w2_s, w2_rows, 4, 8)
-        load_weights(w1_w, w1_words, 2, 2, "w1")
         load_weights(w1t_w, w1t_words, 0, 2, "w1t")
         load_scales(w1t_s, w1t_rows, 0, 6)
+        load_weights(w1_w, w1_words, 2, 4, "w1")
         load_weights(w2_w, w2t_words, 4, 2, "w2")
-        load_weights(w1_w, w1_words, 4, 2, "w1")
         load_weights(w1t_w, w1t_words, 2, 4, "w1t")
 
-        nc.scalar.dma_start(out=gate_rows[0:E, :], in_=gate[0:1, :].rearrange("o (e c) -> (o e) c", c=C))
         gate_ps = psum.tile([P, 2, P], F32, name="gate_ps", tag="da_t")
         nc.tensor.transpose(gate_ps[:, 0, :], gate_rows[:], ident[:])
         gate2 = keep.tile([P, 8], F32, name="gate2")
@@ -105,16 +103,16 @@ def tile_moe_rec_mlp_relu2_kernel(
         windows = [keep.tile([P, T], F32, name="window_%d" % t) for t in range(PACK)]
 
         def gather(e):
-            piece = offsets[:, e * C // LIST_ROWS : (e + 1) * C // LIST_ROWS]
+            piece = offsets[:, e * GROUP * C // LIST_ROWS : (e + 1) * GROUP * C // LIST_ROWS]
             tables = [(dy_tab[:, 0, :], dys_tab[:, 0, :]), (dy_tab[:, 1, :], dys_tab[:, 1, :]), (x_tab[:], xs_tab[:, 0, :])]
             got = []
             for n, (words, scales) in enumerate(tables):
-                w = picked.tile([P, C], U32, name="words_%d" % n, align_bytes=64)
+                w = picked.tile([P, GROUP * C], U32, name="words_%d" % n, align_bytes=64)
                 nc.vector.tensor_copy(w[:], words.bitcast(U32).indirect(piece))
-                s = picked.tile([P, C], U8, name="scales_%d" % n, align_bytes=64)
+                s = picked.tile([P, GROUP * C], U8, name="scales_%d" % n, align_bytes=64)
                 nc.vector.tensor_copy(s[:], scales.indirect(piece))
-                got.append((w, s))
-            return got
+                got.append([(w[:, u * C : (u + 1) * C], s[:, u * C : (u + 1) * C]) for u in range(GROUP)])
+            return [[pair[u] for pair in got] for u in range(GROUP)]
 
         def product(out, lhs, weight, weight_scales, start, stop):
             nc.tensor.matmul_mx(
@@ -160,27 +158,28 @@ def tile_moe_rec_mlp_relu2_kernel(
             piece = offsets[:, first * C // LIST_ROWS : (last + 1) * C // LIST_ROWS]
             nc.vector.tensor_copy(windows[t][:].indirect(piece), dx[:, t, first * C : (last + 1) * C])
 
-        tail_from = [E - 1 - t for t in range(PACK)]
+        tail_from = [5,5,4,3]
         got, da, da_q = {}, {}, {}
-        for e in range(AHEAD):
-            got[e] = gather(e)
+        for g in range(AHEAD):
+            got.update(enumerate(gather(g), g * GROUP))
         for step in range(E + 2):
             if step < E:
                 da[step] = hidden(step)
-            if step + AHEAD < E:
-                got[step + AHEAD] = gather(step + AHEAD)
+            g, u = divmod(step, GROUP)
+            if u == GROUP - 1 and g + AHEAD < GROUPS:
+                got.update(enumerate(gather(g + AHEAD), (g + AHEAD) * GROUP))
             if 0 <= step - 1 < E:
                 da_q[step - 1] = quantise(da[step - 1])
             if 0 <= step - 2 < E:
                 back(step - 2, da_q[step - 2])
             e = step - 3
             for t in range(PACK):
-                alone = t < ALONE
-                if e == 0 and alone:
-                    scatter(t, 0, 0)
-                elif e == tail_from[t] - 1:
-                    scatter(t, 1 if alone else 0, e)
+                if 0 <= e < tail_from[t]:
+                    if (e + t // 2) % 2 == 1 and e + 1 < tail_from[t]:
+                        continue
+                    scatter(t, e - 1 if (e + t // 2) % 2 == 0 and e > 0 else e, e)
 
+        pairs = keep.tile([P, 2, T, 2], BF16, name="pairs", align_bytes=64)
         rounded = keep.tile([P, T, PACK], BF16, name="rounded", align_bytes=64)
         y_codes = keep.tile([P, T * PACK], U8, name="y_codes", align_bytes=64)
         y_scales = keep.tile([P, T], U8, name="y_scales", align_bytes=64)
@@ -188,18 +187,24 @@ def tile_moe_rec_mlp_relu2_kernel(
         for t in range(PACK):
             scatter(t, tail_from[t], E - 1)
             nc.sync.dma_start(out=out_rows[:, t, :], in_=windows[t][:])
+            u, v = divmod(t, 2)
             if t < 2:
-                nc.scalar.copy(rounded[:, :, t], windows[t][:])
+                nc.scalar.copy(pairs[:, u, :, v], windows[t][:])
             elif t == 2:
-                nc.scalar.copy(rounded[:, :VECTOR_COLS, 2:4], windows[t][:, :VECTOR_COLS].unsqueeze(2).to_broadcast([P, VECTOR_COLS, 2]))
-                nc.scalar.copy(rounded[:, VECTOR_COLS:, t], windows[t][:, VECTOR_COLS:])
+                nc.scalar.copy(pairs[:, u, :VECTOR_COLS, :], windows[t][:, :VECTOR_COLS].unsqueeze(2).to_broadcast([P, VECTOR_COLS, 2]))
+                nc.scalar.copy(pairs[:, u, VECTOR_COLS:, v], windows[t][:, VECTOR_COLS:])
             else:
-                nc.scalar.copy(rounded[:, VECTOR_COLS:, t], windows[t][:, VECTOR_COLS:])
+                nc.scalar.copy(pairs[:, u, VECTOR_COLS:, v], windows[t][:, VECTOR_COLS:])
                 for a in range(0, VECTOR_COLS, PIECE):
-                    nc.vector.tensor_copy(rounded[:, a : a + PIECE, t], windows[t][:, a : a + PIECE])
+                    nc.vector.tensor_copy(pairs[:, u, a : a + PIECE, v], windows[t][:, a : a + PIECE])
+        pair_words = pairs[:].bitcast(F32).rearrange("p u c o -> p c (u o)")
+        rounded_words = rounded[:].bitcast(F32)
+        nc.scalar.copy(rounded_words[:, VECTOR_COLS:, :], pair_words[:, VECTOR_COLS:, :])
+        for a in range(0, VECTOR_COLS, PIECE):
+            nc.vector.tensor_copy(rounded_words[:, a : a + PIECE, :], pair_words[:, a : a + PIECE, :])
         flat = rounded[:].rearrange("p c t -> p (c t)")
         words_out = out_1[0].rearrange("p c d -> p (c d)")
-        for a in (0, VECTOR_COLS, PIECE):
+        for a in (0, PIECE, VECTOR_COLS):
             b = a + PIECE
             nc.vector.quantize_mx(out=y_codes[:, PACK * a : PACK * b].bitcast(FP8X4), scales=y_scales[:, a:b], in_=flat[:, PACK * a : PACK * b])
             nc.sync.dma_start(out=words_out[:, PACK * a : PACK * b].bitcast(I32), in_=y_codes[:, PACK * a : PACK * b].bitcast(I32))

from contextlib import ExitStack

import concourse.mybir as mybir
from concourse.masks import make_identity

K, T, E, C, H, N = 512, 768, 6, 128, 512, 1024
FLOPS = 2 * E * C * (K * H + N * H + H * K)

F32 = mybir.dt.float32
BF16 = mybir.dt.bfloat16
I32 = mybir.dt.int32
U32 = mybir.dt.uint32
U16 = mybir.dt.uint16
U8 = mybir.dt.uint8
FP8X4 = mybir.dt.float8_e4m3fn_x4
FP4X4 = mybir.dt.float4_e2m1fn_x4
ACT = mybir.ActivationFunctionType
ALU = mybir.AluOpType

P = 128
PACK = 4
QUADS = 4
GROUP = 3
GROUPS = E // GROUP
LIST_ROWS = 16
VECTOR_COLS = 512
PIECE = 256
ALONE = 2
AHEAD = 2


def tile_moe_rec_mlp_relu2_kernel(
    tc, x_words, x_scales, dy_words, dy_scales, w1_words, w1_scales, w2t_words, w2t_scales,
    w1t_words, w1t_scales, gate, offs, out_0, out_1, out_2,
):
    nc = tc.nc
    with ExitStack() as ctx:
        keep = ctx.enter_context(tc.tile_pool(name="keep", bufs=1))
        picked = ctx.enter_context(tc.tile_pool(name="picked", bufs=AHEAD))
        work = ctx.enter_context(tc.tile_pool(name="work", bufs=2))
        psum = ctx.enter_context(tc.psum_pool(name="psum", bufs=1))

        offsets = keep.tile([P, E * C // LIST_ROWS], U16, name="offsets")
        x_tab = keep.tile([P, T], I32, name="x_tab", align_bytes=64)
        dy_tab = keep.tile([P, 2, T], I32, name="dy_tab", align_bytes=64)
        xs_tab = keep.tile([P, 1, T], U8, name="xs_tab", align_bytes=64)
        dys_tab = keep.tile([P, 2, T], U8, name="dys_tab", align_bytes=64)
        w1_s = keep.tile([P, E, H], U8, name="w1_s", align_bytes=64)
        w2_s = keep.tile([P, 2 * E, H], U8, name="w2_s", align_bytes=64)
        w1t_s = keep.tile([P, E, K], U8, name="w1t_s", align_bytes=64)

        for plane in (xs_tab, dys_tab,):
            nc.gpsimd.memset(plane[:].bitcast(I32), 0)
        for plane in (w1_s, w2_s, w1t_s,):
            nc.vector.memset(plane[:].bitcast(I32), 0)

        def load_scales(plane, rows, first, count, queue=nc.sync):
            for r in range(PACK):
                queue.dma_start(
                    out=plane[r:P:32, first : first + count, :].bitcast(I32),
                    in_=rows[r:16:4, first : first + count, :].bitcast(I32),
                )

        def load_weights(held, words, first, count, label):
            passes = words.shape[1]
            tile = keep.tile([P, count * passes, 2 * H], U8, name="%s_%d" % (label, first), align_bytes=64)
            src = words[first : first + count].rearrange("e s p b -> p (e s) b")
            nc.sync.dma_start(out=tile[:].bitcast(I32), in_=src.bitcast(I32))
            for u in range(count):
                held[first + u] = [tile[:, u * passes + s, :] for s in range(passes)]

        nc.sync.dma_start(offsets[:], offs)
        w1_w, w2_w, w1t_w = {}, {}, {}
        w1_rows = w1_scales.rearrange("e s b i -> b (e s) i")
        w2_rows = w2t_scales.rearrange("e s b i -> b (e s) i")
        w1t_rows = w1t_scales.rearrange("e s b i -> b (e s) i")
        load_scales(xs_tab, x_scales.rearrange("s b t -> b s t"), 0, 1)
        nc.sync.dma_start(out=x_tab[:], in_=x_words[0].rearrange("p t d -> p (t d)").bitcast(I32))
        nc.sync.dma_start(out=dy_tab[:], in_=dy_words.rearrange("s p t d -> p s (t d)").bitcast(I32))
        load_scales(dys_tab, dy_scales.rearrange("s b t -> b s t"), 0, 2)
        load_weights(w1_w, w1_words, 0, 2, "w1")
        load_scales(w1_s, w1_rows, 0, 6)
        load_weights(w2_w, w2t_words, 0, 2, "w2")
        load_scales(w2_s, w2_rows, 0, 12)
        gate_rows = keep.tile([P, C], F32, name="gate_rows")
        nc.gpsimd.memset(gate_rows[:], 0.0)
        nc.gpsimd.dma_start(out=gate_rows[0:E, :], in_=gate[0:1, :].rearrange("o (e c) -> (o e) c", c=C))
        ident = keep.tile([P, P], F32, name="ident")
        make_identity(nc, ident[:])
        load_weights(w2_w, w2t_words, 2, 2, "w2")
        load_weights(w1t_w, w1t_words, 0, 2, "w1t")
        load_scales(w1t_s, w1t_rows, 0, 6)
        load_weights(w1_w, w1_words, 2, 4, "w1")
        load_weights(w2_w, w2t_words, 4, 2, "w2")
        load_weights(w1t_w, w1t_words, 2, 4, "w1t")

        gate_ps = psum.tile([P, 2, P], F32, name="gate_ps", tag="da_t")
        nc.tensor.transpose(gate_ps[:, 0, :], gate_rows[:], ident[:])
        gate2 = keep.tile([P, 8], F32, name="gate2")
        nc.scalar.activation(gate2[:], gate_ps[:, 0, 0:8], ACT.Copy, scale=2.0)

        dx = keep.tile([P, PACK, E * C], F32, name="dx")
        windows = [keep.tile([P, T], F32, name="window_%d" % t) for t in range(PACK)]

        def gather(e):
            piece = offsets[:, e * GROUP * C // LIST_ROWS : (e + 1) * GROUP * C // LIST_ROWS]
            tables = [(dy_tab[:, 0, :], dys_tab[:, 0, :]), (dy_tab[:, 1, :], dys_tab[:, 1, :]), (x_tab[:], xs_tab[:, 0, :])]
            got = []
            for n, (words, scales) in enumerate(tables):
                w = picked.tile([P, GROUP * C], U32, name="words_%d" % n, align_bytes=64)
                nc.vector.tensor_copy(w[:], words.bitcast(U32).indirect(piece))
                s = picked.tile([P, GROUP * C], U8, name="scales_%d" % n, align_bytes=64)
                nc.vector.tensor_copy(s[:], scales.indirect(piece))
                got.append([(w[:, u * C : (u + 1) * C], s[:, u * C : (u + 1) * C]) for u in range(GROUP)])
            return [[pair[u] for pair in got] for u in range(GROUP)]

        def product(out, lhs, weight, weight_scales, start, stop):
            nc.tensor.matmul_mx(
                out=out, lhsT=lhs[0][:].bitcast(FP8X4), lhsT_scale=lhs[1][:],
                rhs=weight.bitcast(FP4X4), rhs_scale=weight_scales, start=start, stop=stop,
            )

        def hidden(e):
            dh_ps = psum.tile([P, H], F32, name="dh_ps", bufs=2)
            for s in range(2):
                product(dh_ps[:], got[e][s], w2_w[e][s], w2_s[:, 2 * e + s, :], s == 0, s == 1)
            dh2 = work.tile([P, H], F32, name="dh2", bufs=2)
            nc.scalar.activation(dh2[:], dh_ps[:], ACT.Copy, scale=gate2[:, e : e + 1])
            a_ps = psum.tile([P, H], F32, name="a_ps", bufs=2)
            product(a_ps[:], got[e][2], w1_w[e][0], w1_s[:, e, :], True, True)
            da = work.tile([P, H], BF16, name="da", align_bytes=64)
            nc.vector.scalar_tensor_tensor(da[:], a_ps[:], 0.0, dh2[:], ALU.max, ALU.mult)
            return da

        def quantise(da):
            words = da[:].bitcast(F32)
            da_ps = psum.tile([P, 2, C], F32, name="da_ps", tag="da_t")
            for u in range(2):
                nc.tensor.transpose(da_ps[:, u, :], words[:, u : H // 2 : 2], ident[:])
            grouped = work.tile([P, C * PACK], BF16, name="grouped", align_bytes=64)
            nc.scalar.copy(grouped[:].bitcast(F32).rearrange("p (c u) -> p c u", u=2), da_ps[:].rearrange("p u c -> p c u"))
            codes = work.tile([P, C], U32, name="codes", align_bytes=64)
            scales = work.tile([P, C], U8, name="code_scales", align_bytes=64)
            nc.vector.quantize_mx(out=codes[:].bitcast(FP8X4), scales=scales[:], in_=grouped[:])
            return codes, scales

        def back(e, da_q):
            dxt_ps = psum.tile([P, K], F32, name="dxt_ps", bufs=1)
            product(dxt_ps[:], da_q, w1t_w[e][0], w1t_s[:, e, :], True, True)
            dxt = work.tile([P, PACK, P], F32, name="dxt")
            nc.scalar.copy(dxt[:], dxt_ps[:].rearrange("c (m t) -> c t m", t=PACK))
            dx_ps = psum.tile([P, PACK, C], F32, name="dx_ps", bufs=2)
            for t in range(PACK):
                nc.tensor.transpose(dx_ps[:, t, :], dxt[:, t, :], ident[:])
            nc.scalar.copy(dx[:, :, e * C : (e + 1) * C], dx_ps[:])

        def scatter(t, first, last):
            piece = offsets[:, first * C // LIST_ROWS : (last + 1) * C // LIST_ROWS]
            nc.vector.tensor_copy(windows[t][:].indirect(piece), dx[:, t, first * C : (last + 1) * C])

        tail_from = [5,5,4,3]
        got, da, da_q = {}, {}, {}
        for g in range(AHEAD):
            got.update(enumerate(gather(g), g * GROUP))
        for step in range(E + 2):
            if step < E:
                da[step] = hidden(step)
            g, u = divmod(step, GROUP)
            if u == GROUP - 1 and g + AHEAD < GROUPS:
                got.update(enumerate(gather(g + AHEAD), (g + AHEAD) * GROUP))
            if 0 <= step - 1 < E:
                da_q[step - 1] = quantise(da[step - 1])
            if 0 <= step - 2 < E:
                back(step - 2, da_q[step - 2])
            e = step - 3
            for t in range(PACK):
                if 0 <= e < tail_from[t]:
                    if (e + t // 2) % 2 == 1 and e + 1 < tail_from[t]:
                        continue
                    scatter(t, e - 1 if (e + t // 2) % 2 == 0 and e > 0 else e, e)

        pairs = keep.tile([P, 2, T, 2], BF16, name="pairs", align_bytes=64)
        rounded = keep.tile([P, T, PACK], BF16, name="rounded", align_bytes=64)
        y_codes = keep.tile([P, T * PACK], U8, name="y_codes", align_bytes=64)
        y_scales = keep.tile([P, T], U8, name="y_scales", align_bytes=64)
        out_rows = out_0.rearrange("(p t) c -> p t c", t=PACK)
        for t in range(PACK):
            scatter(t, tail_from[t], E - 1)
            nc.sync.dma_start(out=out_rows[:, t, :], in_=windows[t][:])
            u, v = divmod(t, 2)
            if t < 2:
                nc.scalar.copy(pairs[:, u, :, v], windows[t][:])
            elif t == 2:
                nc.scalar.copy(pairs[:, u, :VECTOR_COLS, :], windows[t][:, :VECTOR_COLS].unsqueeze(2).to_broadcast([P, VECTOR_COLS, 2]))
                nc.scalar.copy(pairs[:, u, VECTOR_COLS:, v], windows[t][:, VECTOR_COLS:])
            else:
                nc.scalar.copy(pairs[:, u, VECTOR_COLS:, v], windows[t][:, VECTOR_COLS:])
                for a in range(0, VECTOR_COLS, PIECE):
                    nc.vector.tensor_copy(pairs[:, u, a : a + PIECE, v], windows[t][:, a : a + PIECE])
        pair_words = pairs[:].bitcast(F32).rearrange("p u c o -> p c (u o)")
        rounded_words = rounded[:].bitcast(F32)
        nc.scalar.copy(rounded_words[:, VECTOR_COLS:, :], pair_words[:, VECTOR_COLS:, :])
        for a in range(0, VECTOR_COLS, PIECE):
            nc.vector.tensor_copy(rounded_words[:, a : a + PIECE, :], pair_words[:, a : a + PIECE, :])
        flat = rounded[:].rearrange("p c t -> p (c t)")
        words_out = out_1[0].rearrange("p c d -> p (c d)")
        for a in (0, PIECE, VECTOR_COLS):
            b = a + PIECE
            nc.vector.quantize_mx(out=y_codes[:, PACK * a : PACK * b].bitcast(FP8X4), scales=y_scales[:, a:b], in_=flat[:, PACK * a : PACK * b])
            nc.sync.dma_start(out=words_out[:, PACK * a : PACK * b].bitcast(I32), in_=y_codes[:, PACK * a : PACK * b].bitcast(I32))
        for q in range(QUADS):
            queue = nc.sync if q % 2 == 0 else nc.scalar
            queue.dma_start(out=out_2[0, q:16:4, :].bitcast(I32), in_=y_scales[q:P:32, :].bitcast(I32))
